import numpy as np
import ml_dtypes


def mxq(x, axis, fmt="e4m3"):
    dtype, down = {"e4m3": (ml_dtypes.float8_e4m3fn, 7), "e5m2": (ml_dtypes.float8_e5m2, 14)}[fmt]
    v = np.moveaxis(np.asarray(x, np.float32).astype(ml_dtypes.bfloat16).astype(np.float64), axis, -1)
    blocks = v.reshape(v.shape[:-1] + (-1, 32))
    amax = np.abs(blocks).max(-1, keepdims=True)
    byte = np.maximum(np.where(amax > 0, np.frexp(amax)[1] - 1 + 127, 0) - down, 1)
    scale = np.exp2(byte - 127.0)
    codes = (blocks / scale).astype(np.float32).astype(dtype).astype(np.float64)
    return np.moveaxis((codes * scale).reshape(v.shape), -1, axis)


WIDE = False


def mx_kscale(k):
    if not WIDE:
        return np.ones(k)
    levels = np.array([10, -10, 5, -5, 0])
    if k % 512:
        return np.exp2(np.random.permutation(np.resize(levels, k // 32))).repeat(32)
    a = np.empty((k // 512, 16))
    for p in range(k // 512):
        a[p, :8] = np.random.permutation(np.resize(levels, 8))
        for g in range(8):
            far = levels[np.abs(levels - a[p, g]) >= 10]
            a[p, g + 8] = far[np.random.randint(len(far))]
    return np.exp2(a.ravel()).repeat(32)


def f64(x):
    return np.asarray(x).astype(np.float64)


def striped(idx):
    return np.tile(idx.reshape(-1, 16).T, (8, 1)).astype(np.uint16)


def unstriped(offs):
    return offs[:16].T.reshape(-1).astype(np.int64)


def relu(v):
    return np.maximum(v, 0.0)


K, T, S, H, N = 1024, 1024, 512, 512, 128


def setup_inputs():
    n = np.random.standard_normal
    s = mx_kscale(K)[:, None]
    u = mx_kscale(H)
    return {
        "xT": (n((K, T)) * s).astype(np.float32),
        "w1": (n((K, H)) / np.sqrt(K) / s).astype(np.float32),
        "w2": (n((H, N)) / np.sqrt(H) / u[:, None]).astype(np.float32),
        "gamma": (np.random.uniform(0.5, 1.5, (H, 1)) * u[:, None]).astype(np.float32),
        "offs": striped(np.random.permutation(T)[:S]),
    }


def reference(xT, w1, w2, gamma, offs):
    xq = mxq(f64(xT)[:, unstriped(offs)], 0, "e4m3")
    h = mxq(f64(w1), 0, "e4m3").T @ xq
    hn = (h - h.mean(axis=1, keepdims=True)) / np.sqrt(h.var(axis=1, keepdims=True) + 1e-5)
    z = relu(f64(gamma) * hn)
    return mxq(f64(w2), 0, "e4m3").T @ mxq(z, 0, "e4m3")

@@ -1,0 +1,188 @@
+from contextlib import ExitStack
+
+import concourse.mybir as mybir
+
+K, T, S, H, N = 1024, 1024, 512, 512, 128
+FLOPS = 2 * K * H * S + 2 * H * N * S
+
+F32 = mybir.dt.float32
+BF16 = mybir.dt.bfloat16
+U32 = mybir.dt.uint32
+U16 = mybir.dt.uint16
+U8 = mybir.dt.uint8
+FP8X4 = mybir.dt.float8_e4m3fn_x4
+ACT = mybir.ActivationFunctionType
+ALU = mybir.AluOpType
+
+P = 128
+PACK = 4
+K_PASS = P * PACK
+EPS = 1e-5
+
+
+def tile_picked_inorm_relu_e_kernel(tc, xT, w1, w2, gamma, offs, out):
+    nc = tc.nc
+    with ExitStack() as ctx:
+        keep = ctx.enter_context(tc.tile_pool(name="keep", bufs=1))
+        psum = ctx.enter_context(tc.psum_pool(name="psum", bufs=1))
+
+        def sb(name, shape, dtype):
+            return keep.tile(shape, dtype, name=name, align_bytes=64)
+
+        def rows(src):
+            return src.rearrange("(p j) c -> p j c", j=PACK)
+
+        def weave(engine, dst, src):
+            o = dst.rearrange("p (c i j) -> p c j i", i=4, j=PACK)
+            s = src.rearrange("p j (c i) -> p c j i", i=4)
+            if engine == "v":
+                nc.vector.tensor_copy(out=o, in_=s)
+            else:
+                nc.scalar.activation(out=o, in_=s, func=ACT.Copy)
+
+        def quantize(codes, scales, woven):
+            nc.vector.quantize_mx(out=codes.bitcast(FP8X4), scales=scales, in_=woven)
+
+        offsets = keep.tile([P, S // 16], U16, name="offsets")
+        x0 = sb("x0", [P, PACK, T], F32)
+        x1 = [sb("x1_%d" % h, [P, PACK, T // 2], F32) for h in range(2)]
+        w1_raw = [sb("w1_raw%d" % g, [P, PACK, H], F32) for g in range(2)]
+        w2_raw = sb("w2_raw", [P, PACK, N], F32)
+        gam = sb("gam", [P, PACK], F32)
+        nc.sync.dma_start(out=x0[:], in_=rows(xT[0:K_PASS, :]))
+        nc.sync.dma_start(offsets[:], offs)
+        for h in range(2):
+            nc.sync.dma_start(out=x1[h][:], in_=rows(xT[K_PASS:K, h * 512 : (h + 1) * 512]))
+        nc.sync.dma_start(out=gam[:], in_=gamma.rearrange("(p j) o -> p (j o)", j=PACK))
+        for g in range(2):
+            nc.sync.dma_start(out=w1_raw[g][:], in_=rows(w1[g * K_PASS : (g + 1) * K_PASS, :]))
+        nc.sync.dma_start(out=w2_raw[:], in_=rows(w2))
+
+        one = sb("one", [P, 1], F32)
+        nc.vector.memset(one[:], 1.0)
+        warm = sb("warm", [P, 1], F32)
+        nc.scalar.activation(out=warm[:], in_=one[:], func=ACT.Abs_reciprocal_sqrt)
+        x_scales = sb("x_scales", [P, T], U8)
+        nc.gpsimd.memset(x_scales[:], 0)
+
+        x_codes = [sb("x_codes%d" % g, [P, T], U32) for g in range(2)]
+        xg_codes = [sb("xg_codes%d" % g, [P, S], U32) for g in range(2)]
+        xg_scales = sb("xg_scales", [P, S], U8)
+
+        xw0 = sb("xw0", [P, PACK * T], BF16)
+        for eng, a, b in (("v", 0, 512), ("s", 512, 768), ("s", 768, 1024)):
+            weave(eng, xw0[:, 4 * a : 4 * b], x0[:, :, a:b])
+        for a, b in ((0, 512), (512, 768), (768, 1024)):
+            quantize(x_codes[0][:, a:b], x_scales[:, a:b], xw0[:, 4 * a : 4 * b])
+        nc.vector.tensor_copy(out=xg_codes[0][:], in_=x_codes[0][:].indirect(offsets[:]))
+
+        xw1 = sb("xw1", [P, PACK * T], BF16)
+        weave("s", xw1[:, 0 : 4 * 256], x1[0][:, :, 0:256])
+        weave("s", xw1[:, 4 * 256 : 4 * 512], x1[0][:, :, 256:512])
+        quantize(x_codes[1][:, 0:256], x_scales[4:P, 0:256], xw1[:, 0:1024])
+        shift = sb("shift", [P, 2 * PACK], F32)
+        half_neg_gam = sb("half_neg_gam", [P, PACK], F32)
+        nc.vector.tensor_copy(out=shift[:].rearrange("p (t e) -> p t e", e=2)[:, :, 0], in_=gam[:])
+        nc.vector.tensor_scalar(out=half_neg_gam[:], in0=gam[:], scalar1=-0.5, scalar2=None, op0=ALU.mult)
+        weave("v", xw1[:, 4 * 512 : 4 * 832], x1[1][:, :, 0:320])
+        weave("s", xw1[:, 4 * 832 : 4 * 1024], x1[1][:, :, 320:512])
+        for a, b in ((256, 512), (512, 768), (768, 1024)):
+            quantize(x_codes[1][:, a:b], x_scales[4:P, a:b], xw1[:, 4 * a : 4 * b])
+        nc.vector.tensor_copy(out=xg_scales[:], in_=x_scales[:].indirect(offsets[:]))
+
+        w_codes = [[sb("w_codes%d_%d" % (g, u), [P, 2 * P], U32) for u in range(2)] for g in range(2)]
+        w_scales = [[sb("w_scales%d_%d" % (g, u), [P, 2 * P], U8) for u in range(2)] for g in range(2)]
+        w_woven = [[sb("w_woven%d_%d" % (g, u), [P, 2 * K_PASS], BF16) for u in range(2)] for g in range(2)]
+
+        def weave_w1(engine, g, u):
+            o = w_woven[g][u][:].rearrange("p (t m j) -> p m j t", t=2, j=PACK)
+            s = w1_raw[g][:].rearrange("p j (m t) -> p m j t", t=PACK)[:, :, :, 2 * u : 2 * u + 2]
+            if engine == "v":
+                nc.vector.tensor_copy(out=o, in_=s)
+            else:
+                nc.scalar.activation(out=o, in_=s, func=ACT.Copy)
+
+        h_ps = [psum.tile([P, S], F32, name="h_ps%d" % t) for t in range(PACK)]
+
+        def first_product(g, t):
+            u, cols = t // 2, slice((t % 2) * P, (t % 2 + 1) * P)
+            nc.tensor.matmul_mx(
+                out=h_ps[t][:],
+                lhsT=w_codes[g][u][:, cols].bitcast(FP8X4),
+                lhsT_scale=w_scales[g][u][:, cols],
+                rhs=xg_codes[g][:].bitcast(FP8X4),
+                rhs_scale=xg_scales[4 * g : P, :],
+                start=(g == 0),
+                stop=(g == 1),
+            )
+
+        nc.vector.tensor_copy(out=xg_codes[1][:], in_=x_codes[1][:].indirect(offsets[:]))
+        warm_ps = psum.tile([P, S], F32, name="warm_ps")
+        for r in range(2):
+            nc.tensor.matmul_mx(out=warm_ps[:], lhsT=xg_codes[0][:, 0:P].bitcast(FP8X4), lhsT_scale=xg_scales[:, 0:P],
+                                rhs=xg_codes[0][:].bitcast(FP8X4), rhs_scale=xg_scales[:], start=True, stop=True)
+        for u in range(2):
+            weave_w1("s", 0, u)
+            quantize(w_codes[0][u][:], w_scales[0][u][:], w_woven[0][u][:])
+        for t in range(PACK):
+            first_product(0, t)
+        weave_w1("v", 1, 0)
+        weave_w1("s", 1, 1)
+        for t in range(PACK):
+            u, e = t // 2, t % 2
+            quantize(w_codes[1][u][:, e * P : (e + 1) * P], w_scales[1][u][:, e * P : (e + 1) * P],
+                     w_woven[1][u][:, e * K_PASS : (e + 1) * K_PASS])
+            first_product(1, t)
+
+        w2_woven = sb("w2_woven", [P, PACK * N], BF16)
+        w2_codes = sb("w2_codes", [P, N], U32)
+        w2_scales = sb("w2_scales", [P, N], U8)
+        weave("s", w2_woven[:], w2_raw[:])
+
+        z_rows = sb("z_rows", [P, PACK, S], BF16)
+        affine = [sb("affine%d" % t, [P, 2], F32) for t in range(PACK)]
+        for t in range(PACK):
+            partial = sb("partial%d" % t, [P, 6], F32)
+            moments = sb("moments%d" % t, [P, 2], F32)
+            rstd = sb("rstd%d" % t, [P, 1], F32)
+            nc.vector.bn_stats(out=partial[:], in_=h_ps[t][:])
+            nc.vector.bn_aggr(out=moments[:], in_=partial[:])
+            nc.vector.tensor_scalar(out=shift[:, 2 * t + 1 : 2 * t + 2], in0=partial[:, 1:2], scalar1=partial[:, 4:5],
+                                    scalar2=half_neg_gam[:, t : t + 1], op0=ALU.add, op1=ALU.mult)
+            nc.scalar.activation(out=rstd[:], in_=moments[:, 1:2], func=ACT.Abs_reciprocal_sqrt, bias=EPS)
+            nc.scalar.activation(out=affine[t][:], in_=shift[:, 2 * t : 2 * t + 2], func=ACT.Copy, scale=rstd[:])
+        for t in range(PACK):
+            if t % 2 == 0:
+                nc.scalar.activation(out=z_rows[:, t, :], in_=h_ps[t][:], func=ACT.Relu,
+                                     scale=affine[t][:, 0:1], bias=affine[t][:, 1:2])
+            else:
+                nc.vector.tensor_scalar(out=z_rows[:, t, :], in0=h_ps[t][:], scalar1=affine[t][:, 0:1],
+                                        scalar2=affine[t][:, 1:2], op0=ALU.mult, op1=ALU.add)
+        quantize(w2_codes[:], w2_scales[:], w2_woven[:])
+
+        z_woven = sb("z_woven", [P, PACK * S], BF16)
+
+        def weave_z(engine, a, b):
+            o = z_woven[:, 4 * a : 4 * b].rearrange("p (c i j) -> p c j i", i=4, j=PACK)
+            s = z_rows[:, :, a:b].rearrange("p j (c i) -> p c j i", i=4)
+            if engine == "v":
+                nc.vector.tensor_scalar(out=o, in0=s, scalar1=0.0, scalar2=None, op0=ALU.max)
+            else:
+                nc.scalar.activation(out=o, in_=s, func=ACT.Relu)
+
+        weave_z("v", 0, 256)
+        weave_z("v", 256, 352)
+        weave_z("s", 352, 512)
+        for h in range(2):
+            z_codes = sb("z_codes%d" % h, [P, 256], U32)
+            z_scales = sb("z_scales%d" % h, [P, 256], U8)
+            o_ps = psum.tile([P, 256], F32, name="o_ps%d" % h)
+            o_sb = sb("o_sb%d" % h, [P, 256], F32)
+            quantize(z_codes[:], z_scales[:], z_woven[:, 1024 * h : 1024 * (h + 1)])
+            nc.tensor.matmul_mx(out=o_ps[:], lhsT=w2_codes[:].bitcast(FP8X4), lhsT_scale=w2_scales[:],
+                                rhs=z_codes[:].bitcast(FP8X4), rhs_scale=z_scales[:], start=True, stop=True)
+            if h == 0:
+                nc.scalar.copy(out=o_sb[:], in_=o_ps[:])
+            else:
+                nc.vector.tensor_copy(out=o_sb[:], in_=o_ps[:])
+            nc.sync.dma_start(out=out[:, 256 * h : 256 * (h + 1)], in_=o_sb[:])

@@ -40,20 +40,29 @@ def tile_picked_inorm_relu_e_kernel(tc, xT, w1, w2, gamma, offs, out):
             else:
                 nc.scalar.activation(out=o, in_=s, func=ACT.Copy)
 
+        def weave_pair(engine, dst, src, u):
+            o = dst.rearrange("p (c i j) -> p c j i", i=4, j=PACK)[:, :, 2 * u : 2 * u + 2, :]
+            s = src.rearrange("p j (c i) -> p c j i", i=4)
+            if engine == "v":
+                nc.vector.tensor_copy(out=o, in_=s)
+            else:
+                nc.scalar.activation(out=o, in_=s, func=ACT.Copy)
+
         def quantize(codes, scales, woven):
             nc.vector.quantize_mx(out=codes.bitcast(FP8X4), scales=scales, in_=woven)
 
         offsets = keep.tile([P, S // 16], U16, name="offsets")
-        x0 = sb("x0", [P, PACK, T], F32)
+        x0 = [sb("x0_%d" % u, [P, 2, T], F32) for u in range(2)]
         x1 = [sb("x1_%d" % h, [P, PACK, T // 2], F32) for h in range(2)]
         w1_raw = [sb("w1_raw%d" % g, [P, PACK, H], F32) for g in range(2)]
         w2_raw = sb("w2_raw", [P, PACK, N], F32)
         gam = sb("gam", [P, PACK], F32)
-        nc.sync.dma_start(out=x0[:], in_=rows(xT[0:K_PASS, :]))
+        for u in range(2):
+            nc.sync.dma_start(out=x0[u][:], in_=rows(xT[0:K_PASS, :])[:, 2 * u : 2 * u + 2, :])
         nc.sync.dma_start(offsets[:], offs)
         for h in range(2):
             nc.sync.dma_start(out=x1[h][:], in_=rows(xT[K_PASS:K, h * 512 : (h + 1) * 512]))
-        nc.sync.dma_start(out=gam[:], in_=gamma.rearrange("(p j) o -> p (j o)", j=PACK))
+        nc.scalar.dma_start(out=gam[:], in_=gamma.rearrange("(p j) o -> p (j o)", j=PACK))
         for g in range(2):
             nc.sync.dma_start(out=w1_raw[g][:], in_=rows(w1[g * K_PASS : (g + 1) * K_PASS, :]))
         nc.sync.dma_start(out=w2_raw[:], in_=rows(w2))
@@ -69,9 +78,14 @@ def tile_picked_inorm_relu_e_kernel(tc, xT, w1, w2, gamma, offs, out):
         xg_codes = [sb("xg_codes%d" % g, [P, S], U32) for g in range(2)]
         xg_scales = sb("xg_scales", [P, S], U8)
 
+        shift = sb("shift", [P, 2 * PACK], F32)
+        half_neg_gam = sb("half_neg_gam", [P, PACK], F32)
+        nc.vector.tensor_copy(out=shift[:].rearrange("p (t e) -> p t e", e=2)[:, :, 0], in_=gam[:])
+        nc.vector.tensor_scalar(out=half_neg_gam[:], in0=gam[:], scalar1=-0.5, scalar2=None, op0=ALU.mult)
+
         xw0 = sb("xw0", [P, PACK * T], BF16)
-        for eng, a, b in (("v", 0, 512), ("s", 512, 768), ("s", 768, 1024)):
-            weave(eng, xw0[:, 4 * a : 4 * b], x0[:, :, a:b])
+        for u, eng, a, b in ((0, "v", 0, 640), (0, "s", 640, 1024), (1, "v", 0, 512), (1, "s", 512, 768), (1, "s", 768, 1024)):
+            weave_pair(eng, xw0[:, 4 * a : 4 * b], x0[u][:, :, a:b], u)
         for a, b in ((0, 512), (512, 768), (768, 1024)):
             quantize(x_codes[0][:, a:b], x_scales[:, a:b], xw0[:, 4 * a : 4 * b])
         nc.vector.tensor_copy(out=xg_codes[0][:], in_=x_codes[0][:].indirect(offsets[:]))
@@ -80,12 +94,8 @@ def tile_picked_inorm_relu_e_kernel(tc, xT, w1, w2, gamma, offs, out):
         weave("s", xw1[:, 0 : 4 * 256], x1[0][:, :, 0:256])
         weave("s", xw1[:, 4 * 256 : 4 * 512], x1[0][:, :, 256:512])
         quantize(x_codes[1][:, 0:256], x_scales[4:P, 0:256], xw1[:, 0:1024])
-        shift = sb("shift", [P, 2 * PACK], F32)
-        half_neg_gam = sb("half_neg_gam", [P, PACK], F32)
-        nc.vector.tensor_copy(out=shift[:].rearrange("p (t e) -> p t e", e=2)[:, :, 0], in_=gam[:])
-        nc.vector.tensor_scalar(out=half_neg_gam[:], in0=gam[:], scalar1=-0.5, scalar2=None, op0=ALU.mult)
-        weave("v", xw1[:, 4 * 512 : 4 * 832], x1[1][:, :, 0:320])
-        weave("s", xw1[:, 4 * 832 : 4 * 1024], x1[1][:, :, 320:512])
+        weave("v", xw1[:, 4 * 512 : 4 * 768], x1[1][:, :, 0:256])
+        weave("s", xw1[:, 4 * 768 : 4 * 1024], x1[1][:, :, 256:512])
         for a, b in ((256, 512), (512, 768), (768, 1024)):
             quantize(x_codes[1][:, a:b], x_scales[4:P, a:b], xw1[:, 4 * a : 4 * b])
         nc.vector.tensor_copy(out=xg_scales[:], in_=x_scales[:].indirect(offsets[:]))
@@ -176,13 +186,14 @@ def tile_picked_inorm_relu_e_kernel(tc, xT, w1, w2, gamma, offs, out):
         for h in range(2):
             z_codes = sb("z_codes%d" % h, [P, 256], U32)
             z_scales = sb("z_scales%d" % h, [P, 256], U8)
-            o_ps = psum.tile([P, 256], F32, name="o_ps%d" % h)
             o_sb = sb("o_sb%d" % h, [P, 256], F32)
             quantize(z_codes[:], z_scales[:], z_woven[:, 1024 * h : 1024 * (h + 1)])
-            nc.tensor.matmul_mx(out=o_ps[:], lhsT=w2_codes[:].bitcast(FP8X4), lhsT_scale=w2_scales[:],
-                                rhs=z_codes[:].bitcast(FP8X4), rhs_scale=z_scales[:], start=True, stop=True)
-            if h == 0:
-                nc.scalar.copy(out=o_sb[:], in_=o_ps[:])
-            else:
-                nc.vector.tensor_copy(out=o_sb[:], in_=o_ps[:])
+            for e, (a, b) in enumerate([(0, 256)] if h == 0 else [(0, 128), (128, 256)]):
+                o_ps = psum.tile([P, b - a], F32, name="o_ps%d_%d" % (h, e))
+                nc.tensor.matmul_mx(out=o_ps[:], lhsT=w2_codes[:].bitcast(FP8X4), lhsT_scale=w2_scales[:],
+                                    rhs=z_codes[:, a:b].bitcast(FP8X4), rhs_scale=z_scales[:, a:b], start=True, stop=True)
+                if e == h:
+                    nc.scalar.copy(out=o_sb[:, a:b], in_=o_ps[:])
+                else:
+                    nc.vector.tensor_copy(out=o_sb[:, a:b], in_=o_ps[:])
             nc.sync.dma_start(out=out[:, 256 * h : 256 * (h + 1)], in_=o_sb[:])

@@ -78,10 +78,14 @@ def tile_picked_inorm_relu_e_kernel(tc, xT, w1, w2, gamma, offs, out):
         xg_codes = [sb("xg_codes%d" % g, [P, S], U32) for g in range(2)]
         xg_scales = sb("xg_scales", [P, S], U8)
 
-        shift = sb("shift", [P, 2 * PACK], F32)
+        shift = [sb("shift%d" % t, [P, 3], F32) for t in range(PACK)]
         half_neg_gam = sb("half_neg_gam", [P, PACK], F32)
-        nc.vector.tensor_copy(out=shift[:].rearrange("p (t e) -> p t e", e=2)[:, :, 0], in_=gam[:])
-        nc.vector.tensor_scalar(out=half_neg_gam[:], in0=gam[:], scalar1=-0.5, scalar2=None, op0=ALU.mult)
+        per_sum = sb("per_sum", [P, 2], F32)
+        for t in range(PACK):
+            nc.vector.tensor_copy(out=shift[t][:, 0:1], in_=gam[:, t : t + 1])
+        nc.vector.tensor_scalar(out=half_neg_gam[:], in0=gam[:], scalar1=-0.5, scalar2=0.0, op0=ALU.mult, op1=ALU.add)
+        nc.vector.memset(per_sum[:, 1:2], -1.0 / S)
+        nc.vector.tensor_scalar(out=per_sum[:, 0:1], in0=gam[:, 0:1], scalar1=-1.0 / S, scalar2=0.0, op0=ALU.mult, op1=ALU.add)
 
         xw0 = sb("xw0", [P, PACK * T], BF16)
         for u, eng, a, b in ((0, "v", 0, 640), (0, "s", 640, 1024), (1, "v", 0, 512), (1, "s", 512, 768), (1, "s", 768, 1024)):
@@ -149,46 +153,60 @@ def tile_picked_inorm_relu_e_kernel(tc, xT, w1, w2, gamma, offs, out):
         w2_scales = sb("w2_scales", [P, N], U8)
         weave("s", w2_woven[:], w2_raw[:])
 
-        z_rows = sb("z_rows", [P, PACK, S], BF16)
+        z_rows = [sb("z_rows%d" % h, [P, PACK, S // 2], BF16) for h in range(2)]
         affine = [sb("affine%d" % t, [P, 2], F32) for t in range(PACK)]
-        for t in range(PACK):
+        rstd = [sb("rstd%d" % t, [P, 1], F32) for t in range(PACK)]
+        h0 = sb("h0", [P, S], F32)
+        squares = sb("squares", [P, S], BF16)
+        total = sb("total", [P, 1], F32)
+        spread = sb("spread", [P, 1], F32)
+        nc.scalar.activation(out=h0[:], in_=h_ps[0][:], func=ACT.Identity, accum_out=total[:])
+        nc.scalar.activation(out=shift[0][:, 1:3], in_=per_sum[:], func=ACT.Copy, scale=total[:])
+        nc.scalar.activation(out=squares[:], in_=h0[:], func=ACT.Square, bias=shift[0][:, 2:3], accum_out=spread[:])
+        nc.scalar.activation(out=rstd[0][:], in_=spread[:], func=ACT.Abs_reciprocal_sqrt, scale=1.0 / S, bias=EPS)
+        for t in range(1, PACK):
             partial = sb("partial%d" % t, [P, 6], F32)
             moments = sb("moments%d" % t, [P, 2], F32)
-            rstd = sb("rstd%d" % t, [P, 1], F32)
             nc.vector.bn_stats(out=partial[:], in_=h_ps[t][:])
             nc.vector.bn_aggr(out=moments[:], in_=partial[:])
-            nc.vector.tensor_scalar(out=shift[:, 2 * t + 1 : 2 * t + 2], in0=partial[:, 1:2], scalar1=partial[:, 4:5],
+            nc.vector.tensor_scalar(out=shift[t][:, 1:2], in0=partial[:, 1:2], scalar1=partial[:, 4:5],
                                     scalar2=half_neg_gam[:, t : t + 1], op0=ALU.add, op1=ALU.mult)
-            nc.scalar.activation(out=rstd[:], in_=moments[:, 1:2], func=ACT.Abs_reciprocal_sqrt, bias=EPS)
-            nc.scalar.activation(out=affine[t][:], in_=shift[:, 2 * t : 2 * t + 2], func=ACT.Copy, scale=rstd[:])
+            nc.scalar.activation(out=rstd[t][:], in_=moments[:, 1:2], func=ACT.Abs_reciprocal_sqrt, bias=EPS)
         for t in range(PACK):
-            if t % 2 == 0:
-                nc.scalar.activation(out=z_rows[:, t, :], in_=h_ps[t][:], func=ACT.Relu,
-                                     scale=affine[t][:, 0:1], bias=affine[t][:, 1:2])
+            if t < 2:
+                nc.scalar.activation(out=affine[t][:], in_=shift[t][:, 0:2], func=ACT.Copy, scale=rstd[t][:])
             else:
-                nc.vector.tensor_scalar(out=z_rows[:, t, :], in0=h_ps[t][:], scalar1=affine[t][:, 0:1],
-                                        scalar2=affine[t][:, 1:2], op0=ALU.mult, op1=ALU.add)
+                nc.vector.tensor_scalar(out=affine[t][:], in0=shift[t][:, 0:2], scalar1=rstd[t][:], scalar2=None, op0=ALU.mult)
+        for t in range(PACK):
+            for h in range(2):
+                cols = slice(h * 256, (h + 1) * 256)
+                if t in (1, 2):
+                    nc.scalar.activation(out=z_rows[h][:, t, :], in_=h_ps[t][:, cols], func=ACT.Relu,
+                                         scale=affine[t][:, 0:1], bias=affine[t][:, 1:2])
+                else:
+                    nc.vector.tensor_scalar(out=z_rows[h][:, t, :], in0=(h0 if t == 0 else h_ps[t])[:, cols],
+                                            scalar1=affine[t][:, 0:1], scalar2=affine[t][:, 1:2], op0=ALU.mult, op1=ALU.add)
         quantize(w2_codes[:], w2_scales[:], w2_woven[:])
 
         z_woven = sb("z_woven", [P, PACK * S], BF16)
 
-        def weave_z(engine, a, b):
-            o = z_woven[:, 4 * a : 4 * b].rearrange("p (c i j) -> p c j i", i=4, j=PACK)
-            s = z_rows[:, :, a:b].rearrange("p j (c i) -> p c j i", i=4)
+        def weave_z(engine, h, a, b):
+            o = z_woven[:, 1024 * h + 4 * a : 1024 * h + 4 * b].rearrange("p (c i j) -> p c j i", i=4, j=PACK)
+            s = z_rows[h][:, :, a:b].rearrange("p j (c i) -> p c j i", i=4)
             if engine == "v":
                 nc.vector.tensor_scalar(out=o, in0=s, scalar1=0.0, scalar2=None, op0=ALU.max)
             else:
                 nc.scalar.activation(out=o, in_=s, func=ACT.Relu)
 
-        weave_z("v", 0, 256)
-        weave_z("v", 256, 352)
-        weave_z("s", 352, 512)
+        weave_z("v", 0, 0, 256)
+        weave_z("v", 1, 0, 128)
+        weave_z("s", 1, 128, 256)
         for h in range(2):
             z_codes = sb("z_codes%d" % h, [P, 256], U32)
             z_scales = sb("z_scales%d" % h, [P, 256], U8)
             o_sb = sb("o_sb%d" % h, [P, 256], F32)
-            quantize(z_codes[:], z_scales[:], z_woven[:, 1024 * h : 1024 * (h + 1)])
             for e, (a, b) in enumerate([(0, 256)] if h == 0 else [(0, 128), (128, 256)]):
+                quantize(z_codes[:, a:b], z_scales[:, a:b], z_woven[:, 1024 * h + 4 * a : 1024 * h + 4 * b])
                 o_ps = psum.tile([P, b - a], F32, name="o_ps%d_%d" % (h, e))
                 nc.tensor.matmul_mx(out=o_ps[:], lhsT=w2_codes[:].bitcast(FP8X4), lhsT_scale=w2_scales[:],
                                     rhs=z_codes[:, a:b].bitcast(FP8X4), rhs_scale=z_scales[:, a:b], start=True, stop=True)

@@ -17,7 +17,16 @@ ALU = mybir.AluOpType
 P = 128
 PACK = 4
 K_PASS = P * PACK
+RUN = 4
+SCALE_ROWS = 4
+HALF_T = T // 2
+HALF_S = S // 2
+QUARTER_T = T // 4
+EIGHTH_T = T // 8
 EPS = 1e-5
+WARM_UP_PASSES = 2
+
+VECTOR_FIRST_ROWS = 640
 
 
 def tile_picked_inorm_relu_e_kernel(tc, xT, w1, w2, gamma, offs, out):
@@ -32,186 +41,192 @@ def tile_picked_inorm_relu_e_kernel(tc, xT, w1, w2, gamma, offs, out):
         def rows(src):
             return src.rearrange("(p j) c -> p j c", j=PACK)
 
-        def weave(engine, dst, src):
-            o = dst.rearrange("p (c i j) -> p c j i", i=4, j=PACK)
-            s = src.rearrange("p j (c i) -> p c j i", i=4)
-            if engine == "v":
-                nc.vector.tensor_copy(out=o, in_=s)
-            else:
-                nc.scalar.activation(out=o, in_=s, func=ACT.Copy)
+        def vector_copy(dst, src):
+            nc.vector.tensor_copy(out=dst, in_=src)
 
-        def weave_pair(engine, dst, src, u):
-            o = dst.rearrange("p (c i j) -> p c j i", i=4, j=PACK)[:, :, 2 * u : 2 * u + 2, :]
-            s = src.rearrange("p j (c i) -> p c j i", i=4)
-            if engine == "v":
-                nc.vector.tensor_copy(out=o, in_=s)
-            else:
-                nc.scalar.activation(out=o, in_=s, func=ACT.Copy)
+        def scalar_copy(dst, src):
+            nc.scalar.activation(out=dst, in_=src, func=ACT.Copy)
+
+        def vector_relu(dst, src):
+            nc.vector.tensor_scalar(out=dst, in0=src, scalar1=0.0, scalar2=None, op0=ALU.max)
+
+        def scalar_relu(dst, src):
+            nc.scalar.activation(out=dst, in_=src, func=ACT.Relu)
+
+        def weave(move, woven, first, src, first_row=0):
+            n_rows, width = src.shape[1], src.shape[2]
+            dst = woven[:, PACK * first : PACK * (first + width)].rearrange("p (c i j) -> p c j i", i=RUN, j=PACK)
+            move(dst[:, :, first_row : first_row + n_rows, :], src.rearrange("p j (c i) -> p c j i", i=RUN))
 
         def quantize(codes, scales, woven):
             nc.vector.quantize_mx(out=codes.bitcast(FP8X4), scales=scales, in_=woven)
 
+        def product(acc, lhs_codes, lhs_scales, rhs_codes, rhs_scales, start=True, stop=True):
+            nc.tensor.matmul_mx(out=acc, lhsT=lhs_codes.bitcast(FP8X4), lhsT_scale=lhs_scales,
+                                rhs=rhs_codes.bitcast(FP8X4), rhs_scale=rhs_scales, start=start, stop=stop)
+
         offsets = keep.tile([P, S // 16], U16, name="offsets")
-        x0 = [sb("x0_%d" % u, [P, 2, T], F32) for u in range(2)]
-        x1 = [sb("x1_%d" % h, [P, PACK, T // 2], F32) for h in range(2)]
+        x0_raw = [sb("x0_raw%d" % u, [P, 2, T], F32) for u in range(2)]
+        x1_raw = [sb("x1_raw%d" % h, [P, PACK, HALF_T], F32) for h in range(2)]
         w1_raw = [sb("w1_raw%d" % g, [P, PACK, H], F32) for g in range(2)]
         w2_raw = sb("w2_raw", [P, PACK, N], F32)
         gam = sb("gam", [P, PACK], F32)
         for u in range(2):
-            nc.sync.dma_start(out=x0[u][:], in_=rows(xT[0:K_PASS, :])[:, 2 * u : 2 * u + 2, :])
+            nc.sync.dma_start(out=x0_raw[u][:], in_=rows(xT[0:K_PASS, :])[:, 2 * u : 2 * u + 2, :])
         nc.sync.dma_start(offsets[:], offs)
         for h in range(2):
-            nc.sync.dma_start(out=x1[h][:], in_=rows(xT[K_PASS:K, h * 512 : (h + 1) * 512]))
-        nc.scalar.dma_start(out=gam[:], in_=gamma.rearrange("(p j) o -> p (j o)", j=PACK))
+            nc.sync.dma_start(out=x1_raw[h][:], in_=rows(xT[K_PASS:K, h * HALF_T : (h + 1) * HALF_T]))
+        nc.scalar.dma_start(out=gam[:], in_=gamma.rearrange("(p t) o -> p (t o)", t=PACK))
         for g in range(2):
             nc.sync.dma_start(out=w1_raw[g][:], in_=rows(w1[g * K_PASS : (g + 1) * K_PASS, :]))
         nc.sync.dma_start(out=w2_raw[:], in_=rows(w2))
 
-        one = sb("one", [P, 1], F32)
-        nc.vector.memset(one[:], 1.0)
-        warm = sb("warm", [P, 1], F32)
-        nc.scalar.activation(out=warm[:], in_=one[:], func=ACT.Abs_reciprocal_sqrt)
+        per_sum = sb("per_sum", [P, 2], F32)
+        nc.vector.memset(per_sum[:, 1:2], -1.0 / S)
+
+        table_preload = sb("table_preload", [P, 1], F32)
+        nc.scalar.activation(out=table_preload[:], in_=per_sum[:, 1:2], func=ACT.Abs_reciprocal_sqrt)
+
         x_scales = sb("x_scales", [P, T], U8)
         nc.gpsimd.memset(x_scales[:], 0)
 
         x_codes = [sb("x_codes%d" % g, [P, T], U32) for g in range(2)]
-        xg_codes = [sb("xg_codes%d" % g, [P, S], U32) for g in range(2)]
-        xg_scales = sb("xg_scales", [P, S], U8)
+        picked_codes = [sb("picked_codes%d" % g, [P, S], U32) for g in range(2)]
+        picked_scales = sb("picked_scales", [P, S], U8)
 
-        shift = [sb("shift%d" % t, [P, 3], F32) for t in range(PACK)]
+        unscaled = [sb("unscaled%d" % t, [P, 3], F32) for t in range(PACK)]
         half_neg_gam = sb("half_neg_gam", [P, PACK], F32)
-        per_sum = sb("per_sum", [P, 2], F32)
         for t in range(PACK):
-            nc.vector.tensor_copy(out=shift[t][:, 0:1], in_=gam[:, t : t + 1])
-        nc.vector.tensor_scalar(out=half_neg_gam[:], in0=gam[:], scalar1=-0.5, scalar2=0.0, op0=ALU.mult, op1=ALU.add)
-        nc.vector.memset(per_sum[:, 1:2], -1.0 / S)
-        nc.vector.tensor_scalar(out=per_sum[:, 0:1], in0=gam[:, 0:1], scalar1=-1.0 / S, scalar2=0.0, op0=ALU.mult, op1=ALU.add)
+            vector_copy(unscaled[t][:, 0:1], gam[:, t : t + 1])
+        nc.vector.tensor_scalar(out=half_neg_gam[:], in0=gam[:], scalar1=-0.5, scalar2=None, op0=ALU.mult)
+        nc.vector.tensor_scalar(out=per_sum[:, 0:1], in0=gam[:, 0:1], scalar1=-1.0 / S, scalar2=None, op0=ALU.mult)
 
-        xw0 = sb("xw0", [P, PACK * T], BF16)
-        for u, eng, a, b in ((0, "v", 0, 640), (0, "s", 640, 1024), (1, "v", 0, 512), (1, "s", 512, 768), (1, "s", 768, 1024)):
-            weave_pair(eng, xw0[:, 4 * a : 4 * b], x0[u][:, :, a:b], u)
-        for a, b in ((0, 512), (512, 768), (768, 1024)):
-            quantize(x_codes[0][:, a:b], x_scales[:, a:b], xw0[:, 4 * a : 4 * b])
-        nc.vector.tensor_copy(out=xg_codes[0][:], in_=x_codes[0][:].indirect(offsets[:]))
+        def quantize_x(g, woven, first, last):
+            quantize(x_codes[g][:, first:last], x_scales[SCALE_ROWS * g : P, first:last],
+                     woven[:, PACK * first : PACK * last])
 
-        xw1 = sb("xw1", [P, PACK * T], BF16)
-        weave("s", xw1[:, 0 : 4 * 256], x1[0][:, :, 0:256])
-        weave("s", xw1[:, 4 * 256 : 4 * 512], x1[0][:, :, 256:512])
-        quantize(x_codes[1][:, 0:256], x_scales[4:P, 0:256], xw1[:, 0:1024])
-        weave("v", xw1[:, 4 * 512 : 4 * 768], x1[1][:, :, 0:256])
-        weave("s", xw1[:, 4 * 768 : 4 * 1024], x1[1][:, :, 256:512])
-        for a, b in ((256, 512), (512, 768), (768, 1024)):
-            quantize(x_codes[1][:, a:b], x_scales[4:P, a:b], xw1[:, 4 * a : 4 * b])
-        nc.vector.tensor_copy(out=xg_scales[:], in_=x_scales[:].indirect(offsets[:]))
+        x0_woven = sb("x0_woven", [P, PACK * T], BF16)
+        weave(vector_copy, x0_woven, 0, x0_raw[0][:, :, 0:VECTOR_FIRST_ROWS])
+        weave(scalar_copy, x0_woven, VECTOR_FIRST_ROWS, x0_raw[0][:, :, VECTOR_FIRST_ROWS:T])
+        x0_pieces = ((vector_copy, 0, HALF_T), (scalar_copy, HALF_T, 3 * QUARTER_T), (scalar_copy, 3 * QUARTER_T, T))
+        for move, first, last in x0_pieces:
+            weave(move, x0_woven, first, x0_raw[1][:, :, first:last], first_row=2)
+        for move, first, last in x0_pieces:
+            quantize_x(0, x0_woven, first, last)
+        vector_copy(picked_codes[0][:], x_codes[0][:].indirect(offsets[:]))
 
-        w_codes = [[sb("w_codes%d_%d" % (g, u), [P, 2 * P], U32) for u in range(2)] for g in range(2)]
-        w_scales = [[sb("w_scales%d_%d" % (g, u), [P, 2 * P], U8) for u in range(2)] for g in range(2)]
-        w_woven = [[sb("w_woven%d_%d" % (g, u), [P, 2 * K_PASS], BF16) for u in range(2)] for g in range(2)]
+        x1_woven = sb("x1_woven", [P, PACK * T], BF16)
+        weave(scalar_copy, x1_woven, 0, x1_raw[0][:, :, 0:QUARTER_T])
+        weave(scalar_copy, x1_woven, QUARTER_T, x1_raw[0][:, :, QUARTER_T : 3 * EIGHTH_T])
+        quantize_x(1, x1_woven, 0, QUARTER_T)
+        weave(vector_copy, x1_woven, 3 * EIGHTH_T, x1_raw[0][:, :, 3 * EIGHTH_T : HALF_T])
+        weave(vector_copy, x1_woven, HALF_T, x1_raw[1][:, :, 0:QUARTER_T])
+        weave(scalar_copy, x1_woven, 3 * QUARTER_T, x1_raw[1][:, :, QUARTER_T:HALF_T])
+        for first in range(QUARTER_T, T, QUARTER_T):
+            quantize_x(1, x1_woven, first, first + QUARTER_T)
+        vector_copy(picked_scales[:], x_scales[:].indirect(offsets[:]))
+        vector_copy(picked_codes[1][:], x_codes[1][:].indirect(offsets[:]))
 
-        def weave_w1(engine, g, u):
-            o = w_woven[g][u][:].rearrange("p (t m j) -> p m j t", t=2, j=PACK)
-            s = w1_raw[g][:].rearrange("p j (m t) -> p m j t", t=PACK)[:, :, :, 2 * u : 2 * u + 2]
-            if engine == "v":
-                nc.vector.tensor_copy(out=o, in_=s)
-            else:
-                nc.scalar.activation(out=o, in_=s, func=ACT.Copy)
+        warm_up = psum.tile([P, S], F32, name="warm_up")
+        for repeat in range(WARM_UP_PASSES):
+            product(warm_up[:], picked_codes[0][:, 0:P], picked_scales[:, 0:P], picked_codes[0][:], picked_scales[:])
 
-        h_ps = [psum.tile([P, S], F32, name="h_ps%d" % t) for t in range(PACK)]
+        early_woven = [sb("early_woven%d" % g, [P, 2 * K_PASS], BF16) for g in range(2)]
+        early_codes = [sb("early_codes%d" % g, [P, 2 * P], U32) for g in range(2)]
+        early_scales = [sb("early_scales%d" % g, [P, 2 * P], U8) for g in range(2)]
+        late_woven = sb("late_woven", [P, 2 * K], BF16)
+        late_codes = [sb("late_codes%d" % e, [P, 2 * P], U32) for e in range(2)]
+        late_scales = [sb("late_scales%d" % e, [P, 2 * P], U8) for e in range(2)]
+        h_psum = [psum.tile([P, S], F32, name="h_psum%d" % t) for t in range(PACK)]
 
-        def first_product(g, t):
-            u, cols = t // 2, slice((t % 2) * P, (t % 2 + 1) * P)
-            nc.tensor.matmul_mx(
-                out=h_ps[t][:],
-                lhsT=w_codes[g][u][:, cols].bitcast(FP8X4),
-                lhsT_scale=w_scales[g][u][:, cols],
-                rhs=xg_codes[g][:].bitcast(FP8X4),
-                rhs_scale=xg_scales[4 * g : P, :],
-                start=(g == 0),
-                stop=(g == 1),
-            )
+        def first_product(g, t, codes, scales, slot):
+            cols = slice(slot * P, (slot + 1) * P)
+            product(h_psum[t][:], codes[:, cols], scales[:, cols], picked_codes[g][:],
+                    picked_scales[SCALE_ROWS * g : P, :], start=(g == 0), stop=(g == 1))
 
-        nc.vector.tensor_copy(out=xg_codes[1][:], in_=x_codes[1][:].indirect(offsets[:]))
-        warm_ps = psum.tile([P, S], F32, name="warm_ps")
-        for r in range(2):
-            nc.tensor.matmul_mx(out=warm_ps[:], lhsT=xg_codes[0][:, 0:P].bitcast(FP8X4), lhsT_scale=xg_scales[:, 0:P],
-                                rhs=xg_codes[0][:].bitcast(FP8X4), rhs_scale=xg_scales[:], start=True, stop=True)
-        for u in range(2):
-            weave_w1("s", 0, u)
-            quantize(w_codes[0][u][:], w_scales[0][u][:], w_woven[0][u][:])
-        for t in range(PACK):
-            first_product(0, t)
-        weave_w1("v", 1, 0)
-        weave_w1("s", 1, 1)
-        for t in range(PACK):
-            u, e = t // 2, t % 2
-            quantize(w_codes[1][u][:, e * P : (e + 1) * P], w_scales[1][u][:, e * P : (e + 1) * P],
-                     w_woven[1][u][:, e * K_PASS : (e + 1) * K_PASS])
-            first_product(1, t)
+        dealt = [w1_raw[g][:].rearrange("p j (m t) -> p m j t", t=PACK) for g in range(2)]
+        early_view = [early_woven[g][:].rearrange("p (t m j) -> p m j t", t=2, j=PACK) for g in range(2)]
+        late_view = late_woven[:].rearrange("p (t g m j) -> p g m j t", t=2, g=2, j=PACK)
+        scalar_copy(early_view[0], dealt[0][:, :, :, 0:2])
+        scalar_copy(late_view[:, 0], dealt[0][:, :, :, 2:4])
+        quantize(early_codes[0][:], early_scales[0][:], early_woven[0][:])
+        for t in range(2):
+            first_product(0, t, early_codes[0], early_scales[0], t)
+        vector_copy(early_view[1], dealt[1][:, :, :, 0:2])
+        scalar_copy(late_view[:, 1], dealt[1][:, :, :, 2:4])
+        for t in range(2):
+            quantize(early_codes[1][:, t * P : (t + 1) * P], early_scales[1][:, t * P : (t + 1) * P],
+                     early_woven[1][:, t * K_PASS : (t + 1) * K_PASS])
+            first_product(1, t, early_codes[1], early_scales[1], t)
+        for e in range(2):
+            quantize(late_codes[e][:], late_scales[e][:], late_woven[:, e * K : (e + 1) * K])
+            for g in range(2):
+                first_product(g, 2 + e, late_codes[e], late_scales[e], g)
 
         w2_woven = sb("w2_woven", [P, PACK * N], BF16)
         w2_codes = sb("w2_codes", [P, N], U32)
         w2_scales = sb("w2_scales", [P, N], U8)
-        weave("s", w2_woven[:], w2_raw[:])
+        weave(scalar_copy, w2_woven, 0, w2_raw[:])
 
-        z_rows = [sb("z_rows%d" % h, [P, PACK, S // 2], BF16) for h in range(2)]
-        affine = [sb("affine%d" % t, [P, 2], F32) for t in range(PACK)]
         rstd = [sb("rstd%d" % t, [P, 1], F32) for t in range(PACK)]
-        h0 = sb("h0", [P, S], F32)
+        h0_sbuf = sb("h0_sbuf", [P, S], F32)
         squares = sb("squares", [P, S], BF16)
-        total = sb("total", [P, 1], F32)
-        spread = sb("spread", [P, 1], F32)
-        nc.scalar.activation(out=h0[:], in_=h_ps[0][:], func=ACT.Identity, accum_out=total[:])
-        nc.scalar.activation(out=shift[0][:, 1:3], in_=per_sum[:], func=ACT.Copy, scale=total[:])
-        nc.scalar.activation(out=squares[:], in_=h0[:], func=ACT.Square, bias=shift[0][:, 2:3], accum_out=spread[:])
-        nc.scalar.activation(out=rstd[0][:], in_=spread[:], func=ACT.Abs_reciprocal_sqrt, scale=1.0 / S, bias=EPS)
+        row_sum = sb("row_sum", [P, 1], F32)
+        square_sum = sb("square_sum", [P, 1], F32)
+        nc.scalar.activation(out=h0_sbuf[:], in_=h_psum[0][:], func=ACT.Identity, accum_out=row_sum[:])
+        nc.scalar.activation(out=unscaled[0][:, 1:3], in_=per_sum[:], func=ACT.Copy, scale=row_sum[:])
+        nc.scalar.activation(out=squares[:], in_=h0_sbuf[:], func=ACT.Square, bias=unscaled[0][:, 2:3],
+                             accum_out=square_sum[:])
+        nc.scalar.activation(out=rstd[0][:], in_=square_sum[:], func=ACT.Abs_reciprocal_sqrt, scale=1.0 / S, bias=EPS)
         for t in range(1, PACK):
             partial = sb("partial%d" % t, [P, 6], F32)
             moments = sb("moments%d" % t, [P, 2], F32)
-            nc.vector.bn_stats(out=partial[:], in_=h_ps[t][:])
+            nc.vector.bn_stats(out=partial[:], in_=h_psum[t][:])
             nc.vector.bn_aggr(out=moments[:], in_=partial[:])
-            nc.vector.tensor_scalar(out=shift[t][:, 1:2], in0=partial[:, 1:2], scalar1=partial[:, 4:5],
+            nc.vector.tensor_scalar(out=unscaled[t][:, 1:2], in0=partial[:, 1:2], scalar1=partial[:, 4:5],
                                     scalar2=half_neg_gam[:, t : t + 1], op0=ALU.add, op1=ALU.mult)
             nc.scalar.activation(out=rstd[t][:], in_=moments[:, 1:2], func=ACT.Abs_reciprocal_sqrt, bias=EPS)
-        for t in range(PACK):
-            if t < 2:
-                nc.scalar.activation(out=affine[t][:], in_=shift[t][:, 0:2], func=ACT.Copy, scale=rstd[t][:])
-            else:
-                nc.vector.tensor_scalar(out=affine[t][:], in0=shift[t][:, 0:2], scalar1=rstd[t][:], scalar2=None, op0=ALU.mult)
-        for t in range(PACK):
+
+        affine = [sb("affine%d" % t, [P, 2], F32) for t in range(PACK)]
+        for t in range(2):
+            nc.scalar.activation(out=affine[t][:], in_=unscaled[t][:, 0:2], func=ACT.Copy, scale=rstd[t][:])
+        for t in range(2, PACK):
+            nc.vector.tensor_scalar(out=affine[t][:], in0=unscaled[t][:, 0:2], scalar1=rstd[t][:], scalar2=None,
+                                    op0=ALU.mult)
+
+        z_rows = [sb("z_rows%d" % h, [P, PACK, HALF_S], BF16) for h in range(2)]
+
+        def vector_normalise(dst, src, t):
+            nc.vector.tensor_scalar(out=dst, in0=src, scalar1=affine[t][:, 0:1], scalar2=affine[t][:, 1:2],
+                                    op0=ALU.mult, op1=ALU.add)
+
+        def scalar_normalise(dst, src, t):
+            nc.scalar.activation(out=dst, in_=src, func=ACT.Relu, scale=affine[t][:, 0:1], bias=affine[t][:, 1:2])
+
+        normalisers = ((vector_normalise, h0_sbuf), (scalar_normalise, h_psum[1]),
+                       (scalar_normalise, h_psum[2]), (vector_normalise, h_psum[3]))
+        for t, (normalise, h_group) in enumerate(normalisers):
             for h in range(2):
-                cols = slice(h * 256, (h + 1) * 256)
-                if t in (1, 2):
-                    nc.scalar.activation(out=z_rows[h][:, t, :], in_=h_ps[t][:, cols], func=ACT.Relu,
-                                         scale=affine[t][:, 0:1], bias=affine[t][:, 1:2])
-                else:
-                    nc.vector.tensor_scalar(out=z_rows[h][:, t, :], in0=(h0 if t == 0 else h_ps[t])[:, cols],
-                                            scalar1=affine[t][:, 0:1], scalar2=affine[t][:, 1:2], op0=ALU.mult, op1=ALU.add)
+                normalise(z_rows[h][:, t, :], h_group[:, h * HALF_S : (h + 1) * HALF_S], t)
         quantize(w2_codes[:], w2_scales[:], w2_woven[:])
 
         z_woven = sb("z_woven", [P, PACK * S], BF16)
-
-        def weave_z(engine, h, a, b):
-            o = z_woven[:, 1024 * h + 4 * a : 1024 * h + 4 * b].rearrange("p (c i j) -> p c j i", i=4, j=PACK)
-            s = z_rows[h][:, :, a:b].rearrange("p j (c i) -> p c j i", i=4)
-            if engine == "v":
-                nc.vector.tensor_scalar(out=o, in0=s, scalar1=0.0, scalar2=None, op0=ALU.max)
-            else:
-                nc.scalar.activation(out=o, in_=s, func=ACT.Relu)
-
-        weave_z("v", 0, 0, 256)
-        weave_z("v", 1, 0, 128)
-        weave_z("s", 1, 128, 256)
-        for h in range(2):
-            z_codes = sb("z_codes%d" % h, [P, 256], U32)
-            z_scales = sb("z_scales%d" % h, [P, 256], U8)
-            o_sb = sb("o_sb%d" % h, [P, 256], F32)
-            for e, (a, b) in enumerate([(0, 256)] if h == 0 else [(0, 128), (128, 256)]):
-                quantize(z_codes[:, a:b], z_scales[:, a:b], z_woven[:, 1024 * h + 4 * a : 1024 * h + 4 * b])
-                o_ps = psum.tile([P, b - a], F32, name="o_ps%d_%d" % (h, e))
-                nc.tensor.matmul_mx(out=o_ps[:], lhsT=w2_codes[:].bitcast(FP8X4), lhsT_scale=w2_scales[:],
-                                    rhs=z_codes[:, a:b].bitcast(FP8X4), rhs_scale=z_scales[:, a:b], start=True, stop=True)
-                if e == h:
-                    nc.scalar.copy(out=o_sb[:, a:b], in_=o_ps[:])
-                else:
-                    nc.vector.tensor_copy(out=o_sb[:, a:b], in_=o_ps[:])
-            nc.sync.dma_start(out=out[:, 256 * h : 256 * (h + 1)], in_=o_sb[:])
+        weave(vector_relu, z_woven, 0, z_rows[0][:])
+        weave(vector_relu, z_woven, HALF_S, z_rows[1][:, :, 0:P])
+        weave(scalar_relu, z_woven, HALF_S + P, z_rows[1][:, :, P:HALF_S])
+        out_pieces = (
+            ((nc.scalar.copy, 0, HALF_S),),
+            ((nc.vector.tensor_copy, 0, P), (nc.scalar.copy, P, HALF_S)),
+        )
+        for h, pieces in enumerate(out_pieces):
+            z_codes = sb("z_codes%d" % h, [P, HALF_S], U32)
+            z_scales = sb("z_scales%d" % h, [P, HALF_S], U8)
+            result = sb("result%d" % h, [P, HALF_S], F32)
+            for copy_out, first, last in pieces:
+                start = h * HALF_S + first
+                quantize(z_codes[:, first:last], z_scales[:, first:last],
+                         z_woven[:, PACK * start : PACK * (start + last - first)])
+                out_psum = psum.tile([P, last - first], F32, name="out_psum%d" % start)
+                product(out_psum[:], w2_codes[:], w2_scales[:], z_codes[:, first:last], z_scales[:, first:last])
+                copy_out(out=result[:, first:last], in_=out_psum[:])
+            nc.sync.dma_start(out=out[:, h * HALF_S : (h + 1) * HALF_S], in_=result[:])

from contextlib import ExitStack

import concourse.mybir as mybir

K, T, S, H, N = 1024, 1024, 512, 512, 128
FLOPS = 2 * K * H * S + 2 * H * N * S

F32 = mybir.dt.float32
BF16 = mybir.dt.bfloat16
U32 = mybir.dt.uint32
U16 = mybir.dt.uint16
U8 = mybir.dt.uint8
FP8X4 = mybir.dt.float8_e4m3fn_x4
ACT = mybir.ActivationFunctionType
ALU = mybir.AluOpType

P = 128
PACK = 4
K_PASS = P * PACK
RUN = 4
SCALE_ROWS = 4
HALF_T = T // 2
HALF_S = S // 2
QUARTER_T = T // 4
EIGHTH_T = T // 8
EPS = 1e-5
WARM_UP_PASSES = 2

VECTOR_FIRST_ROWS = 640


def tile_picked_inorm_relu_e_kernel(tc, xT, w1, w2, gamma, offs, out):
    nc = tc.nc
    with ExitStack() as ctx:
        keep = ctx.enter_context(tc.tile_pool(name="keep", bufs=1))
        psum = ctx.enter_context(tc.psum_pool(name="psum", bufs=1))

        def sb(name, shape, dtype):
            return keep.tile(shape, dtype, name=name, align_bytes=64)

        def rows(src):
            return src.rearrange("(p j) c -> p j c", j=PACK)

        def vector_copy(dst, src):
            nc.vector.tensor_copy(out=dst, in_=src)

        def scalar_copy(dst, src):
            nc.scalar.activation(out=dst, in_=src, func=ACT.Copy)

        def vector_relu(dst, src):
            nc.vector.tensor_scalar(out=dst, in0=src, scalar1=0.0, scalar2=None, op0=ALU.max)

        def scalar_relu(dst, src):
            nc.scalar.activation(out=dst, in_=src, func=ACT.Relu)

        def weave(move, woven, first, src, first_row=0):
            n_rows, width = src.shape[1], src.shape[2]
            dst = woven[:, PACK * first : PACK * (first + width)].rearrange("p (c i j) -> p c j i", i=RUN, j=PACK)
            move(dst[:, :, first_row : first_row + n_rows, :], src.rearrange("p j (c i) -> p c j i", i=RUN))

        def quantize(codes, scales, woven):
            nc.vector.quantize_mx(out=codes.bitcast(FP8X4), scales=scales, in_=woven)

        def product(acc, lhs_codes, lhs_scales, rhs_codes, rhs_scales, start=True, stop=True):
            nc.tensor.matmul_mx(out=acc, lhsT=lhs_codes.bitcast(FP8X4), lhsT_scale=lhs_scales,
                                rhs=rhs_codes.bitcast(FP8X4), rhs_scale=rhs_scales, start=start, stop=stop)

        offsets = keep.tile([P, S // 16], U16, name="offsets")
        x0_raw = [sb("x0_raw%d" % u, [P, 2, T], F32) for u in range(2)]
        x1_raw = [sb("x1_raw%d" % h, [P, PACK, HALF_T], F32) for h in range(2)]
        w1_raw = [sb("w1_raw%d" % g, [P, PACK, H], F32) for g in range(2)]
        w2_raw = sb("w2_raw", [P, PACK, N], F32)
        gam = sb("gam", [P, PACK], F32)
        for u in range(2):
            nc.sync.dma_start(out=x0_raw[u][:], in_=rows(xT[0:K_PASS, :])[:, 2 * u : 2 * u + 2, :])
        nc.sync.dma_start(offsets[:], offs)
        for h in range(2):
            nc.sync.dma_start(out=x1_raw[h][:], in_=rows(xT[K_PASS:K, h * HALF_T : (h + 1) * HALF_T]))
        nc.scalar.dma_start(out=gam[:], in_=gamma.rearrange("(p t) o -> p (t o)", t=PACK))
        for g in range(2):
            nc.sync.dma_start(out=w1_raw[g][:], in_=rows(w1[g * K_PASS : (g + 1) * K_PASS, :]))
        nc.sync.dma_start(out=w2_raw[:], in_=rows(w2))

        per_sum = sb("per_sum", [P, 2], F32)
        nc.vector.memset(per_sum[:, 1:2], -1.0 / S)

        table_preload = sb("table_preload", [P, 1], F32)
        nc.scalar.activation(out=table_preload[:], in_=per_sum[:, 1:2], func=ACT.Abs_reciprocal_sqrt)

        x_scales = sb("x_scales", [P, T], U8)
        nc.gpsimd.memset(x_scales[:], 0)

        x_codes = [sb("x_codes%d" % g, [P, T], U32) for g in range(2)]
        picked_codes = [sb("picked_codes%d" % g, [P, S], U32) for g in range(2)]
        picked_scales = sb("picked_scales", [P, S], U8)

        unscaled = [sb("unscaled%d" % t, [P, 3], F32) for t in range(PACK)]
        half_neg_gam = sb("half_neg_gam", [P, PACK], F32)
        for t in range(PACK):
            vector_copy(unscaled[t][:, 0:1], gam[:, t : t + 1])
        nc.vector.tensor_scalar(out=half_neg_gam[:], in0=gam[:], scalar1=-0.5, scalar2=None, op0=ALU.mult)
        nc.vector.tensor_scalar(out=per_sum[:, 0:1], in0=gam[:, 0:1], scalar1=-1.0 / S, scalar2=None, op0=ALU.mult)

        def quantize_x(g, woven, first, last):
            quantize(x_codes[g][:, first:last], x_scales[SCALE_ROWS * g : P, first:last],
                     woven[:, PACK * first : PACK * last])

        x0_woven = sb("x0_woven", [P, PACK * T], BF16)
        weave(vector_copy, x0_woven, 0, x0_raw[0][:, :, 0:VECTOR_FIRST_ROWS])
        weave(scalar_copy, x0_woven, VECTOR_FIRST_ROWS, x0_raw[0][:, :, VECTOR_FIRST_ROWS:T])
        x0_pieces = ((vector_copy, 0, HALF_T), (scalar_copy, HALF_T, 3 * QUARTER_T), (scalar_copy, 3 * QUARTER_T, T))
        for move, first, last in x0_pieces:
            weave(move, x0_woven, first, x0_raw[1][:, :, first:last], first_row=2)
        for move, first, last in x0_pieces:
            quantize_x(0, x0_woven, first, last)
        vector_copy(picked_codes[0][:], x_codes[0][:].indirect(offsets[:]))

        x1_woven = sb("x1_woven", [P, PACK * T], BF16)
        weave(scalar_copy, x1_woven, 0, x1_raw[0][:, :, 0:QUARTER_T])
        weave(scalar_copy, x1_woven, QUARTER_T, x1_raw[0][:, :, QUARTER_T : 3 * EIGHTH_T])
        quantize_x(1, x1_woven, 0, QUARTER_T)
        weave(vector_copy, x1_woven, 3 * EIGHTH_T, x1_raw[0][:, :, 3 * EIGHTH_T : HALF_T])
        weave(vector_copy, x1_woven, HALF_T, x1_raw[1][:, :, 0:QUARTER_T])
        weave(scalar_copy, x1_woven, 3 * QUARTER_T, x1_raw[1][:, :, QUARTER_T:HALF_T])
        for first in range(QUARTER_T, T, QUARTER_T):
            quantize_x(1, x1_woven, first, first + QUARTER_T)
        vector_copy(picked_scales[:], x_scales[:].indirect(offsets[:]))
        vector_copy(picked_codes[1][:], x_codes[1][:].indirect(offsets[:]))

        warm_up = psum.tile([P, S], F32, name="warm_up")
        for repeat in range(WARM_UP_PASSES):
            product(warm_up[:], picked_codes[0][:, 0:P], picked_scales[:, 0:P], picked_codes[0][:], picked_scales[:])

        early_woven = [sb("early_woven%d" % g, [P, 2 * K_PASS], BF16) for g in range(2)]
        early_codes = [sb("early_codes%d" % g, [P, 2 * P], U32) for g in range(2)]
        early_scales = [sb("early_scales%d" % g, [P, 2 * P], U8) for g in range(2)]
        late_woven = sb("late_woven", [P, 2 * K], BF16)
        late_codes = [sb("late_codes%d" % e, [P, 2 * P], U32) for e in range(2)]
        late_scales = [sb("late_scales%d" % e, [P, 2 * P], U8) for e in range(2)]
        h_psum = [psum.tile([P, S], F32, name="h_psum%d" % t) for t in range(PACK)]

        def first_product(g, t, codes, scales, slot):
            cols = slice(slot * P, (slot + 1) * P)
            product(h_psum[t][:], codes[:, cols], scales[:, cols], picked_codes[g][:],
                    picked_scales[SCALE_ROWS * g : P, :], start=(g == 0), stop=(g == 1))

        dealt = [w1_raw[g][:].rearrange("p j (m t) -> p m j t", t=PACK) for g in range(2)]
        early_view = [early_woven[g][:].rearrange("p (t m j) -> p m j t", t=2, j=PACK) for g in range(2)]
        late_view = late_woven[:].rearrange("p (t g m j) -> p g m j t", t=2, g=2, j=PACK)
        scalar_copy(early_view[0], dealt[0][:, :, :, 0:2])
        scalar_copy(late_view[:, 0], dealt[0][:, :, :, 2:4])
        quantize(early_codes[0][:], early_scales[0][:], early_woven[0][:])
        for t in range(2):
            first_product(0, t, early_codes[0], early_scales[0], t)
        vector_copy(early_view[1], dealt[1][:, :, :, 0:2])
        scalar_copy(late_view[:, 1], dealt[1][:, :, :, 2:4])
        for t in range(2):
            quantize(early_codes[1][:, t * P : (t + 1) * P], early_scales[1][:, t * P : (t + 1) * P],
                     early_woven[1][:, t * K_PASS : (t + 1) * K_PASS])
            first_product(1, t, early_codes[1], early_scales[1], t)
        for e in range(2):
            quantize(late_codes[e][:], late_scales[e][:], late_woven[:, e * K : (e + 1) * K])
            for g in range(2):
                first_product(g, 2 + e, late_codes[e], late_scales[e], g)

        w2_woven = sb("w2_woven", [P, PACK * N], BF16)
        w2_codes = sb("w2_codes", [P, N], U32)
        w2_scales = sb("w2_scales", [P, N], U8)
        weave(scalar_copy, w2_woven, 0, w2_raw[:])

        rstd = [sb("rstd%d" % t, [P, 1], F32) for t in range(PACK)]
        h0_sbuf = sb("h0_sbuf", [P, S], F32)
        squares = sb("squares", [P, S], BF16)
        row_sum = sb("row_sum", [P, 1], F32)
        square_sum = sb("square_sum", [P, 1], F32)
        nc.scalar.activation(out=h0_sbuf[:], in_=h_psum[0][:], func=ACT.Identity, accum_out=row_sum[:])
        nc.scalar.activation(out=unscaled[0][:, 1:3], in_=per_sum[:], func=ACT.Copy, scale=row_sum[:])
        nc.scalar.activation(out=squares[:], in_=h0_sbuf[:], func=ACT.Square, bias=unscaled[0][:, 2:3],
                             accum_out=square_sum[:])
        nc.scalar.activation(out=rstd[0][:], in_=square_sum[:], func=ACT.Abs_reciprocal_sqrt, scale=1.0 / S, bias=EPS)
        for t in range(1, PACK):
            partial = sb("partial%d" % t, [P, 6], F32)
            moments = sb("moments%d" % t, [P, 2], F32)
            nc.vector.bn_stats(out=partial[:], in_=h_psum[t][:])
            nc.vector.bn_aggr(out=moments[:], in_=partial[:])
            nc.vector.tensor_scalar(out=unscaled[t][:, 1:2], in0=partial[:, 1:2], scalar1=partial[:, 4:5],
                                    scalar2=half_neg_gam[:, t : t + 1], op0=ALU.add, op1=ALU.mult)
            nc.scalar.activation(out=rstd[t][:], in_=moments[:, 1:2], func=ACT.Abs_reciprocal_sqrt, bias=EPS)

        affine = [sb("affine%d" % t, [P, 2], F32) for t in range(PACK)]
        for t in range(2):
            nc.scalar.activation(out=affine[t][:], in_=unscaled[t][:, 0:2], func=ACT.Copy, scale=rstd[t][:])
        for t in range(2, PACK):
            nc.vector.tensor_scalar(out=affine[t][:], in0=unscaled[t][:, 0:2], scalar1=rstd[t][:], scalar2=None,
                                    op0=ALU.mult)

        z_rows = [sb("z_rows%d" % h, [P, PACK, HALF_S], BF16) for h in range(2)]

        def vector_normalise(dst, src, t):
            nc.vector.tensor_scalar(out=dst, in0=src, scalar1=affine[t][:, 0:1], scalar2=affine[t][:, 1:2],
                                    op0=ALU.mult, op1=ALU.add)

        def scalar_normalise(dst, src, t):
            nc.scalar.activation(out=dst, in_=src, func=ACT.Relu, scale=affine[t][:, 0:1], bias=affine[t][:, 1:2])

        normalisers = ((vector_normalise, h0_sbuf), (scalar_normalise, h_psum[1]),
                       (scalar_normalise, h_psum[2]), (vector_normalise, h_psum[3]))
        for t, (normalise, h_group) in enumerate(normalisers):
            for h in range(2):
                normalise(z_rows[h][:, t, :], h_group[:, h * HALF_S : (h + 1) * HALF_S], t)
        quantize(w2_codes[:], w2_scales[:], w2_woven[:])

        z_woven = sb("z_woven", [P, PACK * S], BF16)
        weave(vector_relu, z_woven, 0, z_rows[0][:])
        weave(vector_relu, z_woven, HALF_S, z_rows[1][:, :, 0:P])
        weave(scalar_relu, z_woven, HALF_S + P, z_rows[1][:, :, P:HALF_S])
        out_pieces = (
            ((nc.scalar.copy, 0, HALF_S),),
            ((nc.vector.tensor_copy, 0, P), (nc.scalar.copy, P, HALF_S)),
        )
        for h, pieces in enumerate(out_pieces):
            z_codes = sb("z_codes%d" % h, [P, HALF_S], U32)
            z_scales = sb("z_scales%d" % h, [P, HALF_S], U8)
            result = sb("result%d" % h, [P, HALF_S], F32)
            for copy_out, first, last in pieces:
                start = h * HALF_S + first
                quantize(z_codes[:, first:last], z_scales[:, first:last],
                         z_woven[:, PACK * start : PACK * (start + last - first)])
                out_psum = psum.tile([P, last - first], F32, name="out_psum%d" % start)
                product(out_psum[:], w2_codes[:], w2_scales[:], z_codes[:, first:last], z_scales[:, first:last])
                copy_out(out=result[:, first:last], in_=out_psum[:])
            nc.sync.dma_start(out=out[:, h * HALF_S : (h + 1) * HALF_S], in_=result[:])
